import numpy as np
import ml_dtypes


def mxq(x, axis, fmt="e4m3"):
    dtype, down = {"e4m3": (ml_dtypes.float8_e4m3fn, 7), "e5m2": (ml_dtypes.float8_e5m2, 14)}[fmt]
    v = np.moveaxis(np.asarray(x, np.float32).astype(ml_dtypes.bfloat16).astype(np.float64), axis, -1)
    blocks = v.reshape(v.shape[:-1] + (-1, 32))
    amax = np.abs(blocks).max(-1, keepdims=True)
    byte = np.maximum(np.where(amax > 0, np.frexp(amax)[1] - 1 + 127, 0) - down, 1)
    scale = np.exp2(byte - 127.0)
    codes = (blocks / scale).astype(np.float32).astype(dtype).astype(np.float64)
    return np.moveaxis((codes * scale).reshape(v.shape), -1, axis)


WIDE = False


def mx_kscale(k):
    if not WIDE:
        return np.ones(k)
    levels = np.array([10, -10, 5, -5, 0])
    if k % 512:
        return np.exp2(np.random.permutation(np.resize(levels, k // 32))).repeat(32)
    a = np.empty((k // 512, 16))
    for p in range(k // 512):
        a[p, :8] = np.random.permutation(np.resize(levels, 8))
        for g in range(8):
            far = levels[np.abs(levels - a[p, g]) >= 10]
            a[p, g + 8] = far[np.random.randint(len(far))]
    return np.exp2(a.ravel()).repeat(32)


BF16 = ml_dtypes.bfloat16


def bf(x):
    return np.asarray(x, np.float32).astype(BF16)


def f64(x):
    return np.asarray(x).astype(np.float64)


E2M1 = np.array([0.0, 0.5, 1.0, 1.5, 2.0, 3.0, 4.0, 6.0, -0.0, -0.5, -1.0, -1.5, -2.0, -3.0, -4.0, -6.0])


def pack_weight(w, fmt):
    k, n = w.shape
    w = f64(bf(w)).reshape(k // 32, 32, n)
    amax = np.abs(w).max(1)
    if fmt == "e4m3":
        byte = np.frexp(amax)[1] - 1 + 127 - 7
    else:
        mant, ex = np.frexp(amax / 6.0)
        byte = np.where(mant > 0.5, ex, ex - 1) + 127
    byte = np.clip(np.where(amax > 0, byte, 1), 1, 254)
    scaled = (w * np.exp2(127.0 - byte)[:, None, :]).reshape(k, n).astype(np.float32)
    by_word = np.ascontiguousarray(scaled.reshape(k // 512, 128, 4, n).transpose(0, 1, 3, 2))
    if fmt == "e4m3":
        words = by_word.astype(ml_dtypes.float8_e4m3fn).view(np.uint8)
    else:
        c = by_word.astype(ml_dtypes.float4_e2m1fn).view(np.uint8) & 0xF
        words = c[..., 0::2] | (c[..., 1::2] << 4)
    return np.ascontiguousarray(words), np.ascontiguousarray(byte.astype(np.uint8).reshape(k // 512, 16, n))


def unpack_weight(words, scales, fmt):
    g, p, n, _ = words.shape
    if fmt == "e4m3":
        vals = np.ascontiguousarray(words).view(ml_dtypes.float8_e4m3fn).astype(np.float64)
    else:
        nib = np.empty((g, p, n, 4), np.uint8)
        nib[..., 0::2] = words & 0xF
        nib[..., 1::2] = words >> 4
        vals = E2M1[nib]
    vals = vals * np.repeat(np.exp2(scales.astype(np.float64) - 127.0), 8, axis=1)[..., None]
    return vals.transpose(0, 1, 3, 2).reshape(g * 512, n)

def planes(Y):
    n, m = Y.shape
    b = f64(bf(Y)).reshape(n // 32, 32, m)
    amax = np.abs(b).max(1)
    byte = np.clip(np.where(amax > 0, np.frexp(amax)[1] - 1 + 127 - 7, 1), 1, 254)
    codes = (b * np.exp2(127.0 - byte)[:, None, :]).reshape(n, m).astype(np.float32).astype(ml_dtypes.float8_e4m3fn).view(np.uint8)
    words = codes.reshape(n // 512, 128, 4, m).transpose(0, 1, 3, 2)
    return np.ascontiguousarray(words), np.ascontiguousarray(byte.astype(np.uint8).reshape(n // 512, 16, m))


T, D, F, M = 1024, 512, 1024, 512

STEEPNESS = 8.0
THRESHOLD = 0.3


def smooth_jump(h):
    return h * (1.0 / (1.0 + np.exp(-STEEPNESS * (h - THRESHOLD))))


def setup_inputs():
    s = mx_kscale(D)
    t = mx_kscale(T)
    r = mx_kscale(D)
    xc = bf(np.random.standard_normal((T, D)) * s)
    xr = bf(np.random.standard_normal((T, D)) * s)
    we_words, we_scales = pack_weight(np.random.standard_normal((D, F)) / np.sqrt(D) / s[:, None], "e4m3")
    wt = bf((1.0 + 0.1 * np.random.standard_normal(T)) * t)
    g = bf(np.random.standard_normal((T, M)) / np.sqrt(T) / t[:, None])
    wd_words, wd_scales = pack_weight((np.random.standard_normal((F, D)) / np.sqrt(D) * r).T, "e4m3")
    wn_words, wn_scales = pack_weight(np.random.standard_normal((D, M)) / r[:, None], "e4m3")
    return {
        "xc": xc,
        "xr": xr,
        "we_words": we_words,
        "we_scales": we_scales,
        "wt": wt,
        "g": g,
        "wd_words": wd_words,
        "wd_scales": wd_scales,
        "wn_words": wn_words,
        "wn_scales": wn_scales,
    }


def core(xc, xr, we_words, we_scales, wt, g, wd_words, wd_scales, wn_words, wn_scales):
    weq = unpack_weight(we_words, we_scales, "e4m3")
    hc = mxq(f64(xc), 1, "e4m3") @ weq
    hr = mxq(f64(xr), 1, "e4m3") @ weq
    zc = smooth_jump(hc)
    zr = smooth_jump(hr)
    dz = f64(wt)[:, None] * (zr - zc)
    n = mxq(dz, 0, "e4m3").T @ mxq(f64(g), 0, "e4m3")
    v = unpack_weight(wd_words, wd_scales, "e4m3").T @ unpack_weight(wn_words, wn_scales, "e4m3")
    return v * n


def reference(xc, xr, we_words, we_scales, wt, g, wd_words, wd_scales, wn_words, wn_scales):
    R_out = core(xc, xr, we_words, we_scales, wt, g, wd_words, wd_scales, wn_words, wn_scales)
    words, scales = planes(R_out.T)
    return R_out, words, scales

@@ -1,0 +1,415 @@
+from contextlib import ExitStack
+
+import concourse.mybir as mybir
+from concourse.masks import make_identity
+
+F32 = mybir.dt.float32
+BF16 = mybir.dt.bfloat16
+I32 = mybir.dt.int32
+U32 = mybir.dt.uint32
+U8 = mybir.dt.uint8
+FP8X4 = mybir.dt.float8_e4m3fn_x4
+ALU = mybir.AluOpType
+ACT = mybir.ActivationFunctionType
+
+T, D, F, M = 1024, 512, 1024, 512
+FLOPS = 2 * (2 * T * D * F + T * F * M + F * D * M)
+P = 128
+FQ = 256
+H_BUFS = 4
+M_BUFS = 4
+SIG_BUFS = 4
+LEAD = 3
+LAG = 1
+TX, SX = 2, 1
+XC_S = (4, 5, 6, 7)
+TGQ = (11, 15)
+TV, SV = 8, 2
+DQ = 4
+CONV = ("g", "s", "s")
+D_N, D_M0, D_M1, D_C, D_T, D_PC, D_PQ = 1, 2, 3, 3, 6, 7, 8
+SUBV = ()
+
+
+def tile_smoothjumptranscoderedgeattribution_x2_kernel(
+    tc, xc, xr, we_words, we_scales, wt, g, wd_words, wd_scales, wn_words, wn_scales, out_0, out_1, out_2
+):
+    nc = tc.nc
+    with ExitStack() as ctx:
+        keep = ctx.enter_context(tc.tile_pool(name="keep", bufs=1))
+        work = ctx.enter_context(tc.tile_pool(name="work", bufs=3))
+        psum = ctx.enter_context(tc.psum_pool(name="psum", bufs=2))
+        ctx.enter_context(tc.manual_schedule())
+
+        x_raw = {}
+        for grp in (0, 1):
+            for s in (0, 1):
+                x_raw[grp, s] = keep.tile([P, 4, D], BF16, name="x_raw_%d_%d" % (grp, s), align_bytes=64)
+        g_raw = [keep.tile([P, 4, M], BF16, name="g_raw_%d" % i, align_bytes=64) for i in (0, 1)]
+        we_w = keep.tile([P, F], U32, name="we_w", align_bytes=64)
+        we_s = keep.tile([P, F], U8, name="we_s", align_bytes=64)
+        wd_w = keep.tile([P, F], U32, name="wd_w", align_bytes=64)
+        wd_s = keep.tile([P, F], U8, name="wd_s", align_bytes=64)
+        wn_w = keep.tile([P, M], U32, name="wn_w", align_bytes=64)
+        wn_s = keep.tile([P, M], U8, name="wn_s", align_bytes=64)
+        wt_sb = keep.tile([P, 2, 4], BF16, name="wt_sb", align_bytes=64)
+        ident = keep.tile([P, P], F32, name="ident", align_bytes=64)
+        warm = keep.tile([P, 1], F32, name="warm", align_bytes=64)
+        v_sb = keep.tile([P, 8, M], F32, name="v_sb", align_bytes=64)
+        p_scales = keep.tile([P, F], U8, name="p_scales", align_bytes=64)
+        g_codes = [keep.tile([P, M], U32, name="g_codes_%d" % i, align_bytes=64) for i in (0, 1)]
+        g_scales = [keep.tile([P, M], U8, name="g_scales_%d" % i, align_bytes=64) for i in (0, 1)]
+        x_codes = [keep.tile([P, 2 * P], U32, name="x_codes_%d" % i, align_bytes=64) for i in range(8)]
+        x_scales = [keep.tile([P, 2 * P], U8, name="x_scales_%d" % i, align_bytes=64) for i in range(8)]
+
+        nc.vector.memset(we_s[:].bitcast(I32), 0)
+        nc.vector.memset(wd_s[:].bitcast(I32), 0)
+        nc.vector.memset(wn_s[:].bitcast(I32), 0)
+        nc.vector.memset(warm[:], 0.0)
+        nc.scalar.activation(out=warm[:], in_=warm[:], func=ACT.Sigmoid)
+
+        def load_x(grp, s, t0, t1):
+            src = (xc, xr)[s][512 * grp : 512 * grp + 512, :].rearrange("(p t) d -> p t d", t=4)
+            nc.sync.dma_start(out=x_raw[grp, s][:, t0:t1, :], in_=src[:, t0:t1, :])
+
+        def load_words(tile, dram, a, b):
+            src = dram[0].rearrange("p n t -> p (n t)")[:, 4 * a : 4 * b]
+            nc.sync.dma_start(out=tile[:, a:b].bitcast(I32), in_=src.bitcast(I32))
+
+        def load_scales(eng, tile, dram):
+            for q in range(4):
+                eng.dma_start(
+                    out=tile[32 * q : 32 * q + 4, :].bitcast(I32), in_=dram[0, 4 * q : 4 * q + 4, :].bitcast(I32)
+                )
+
+        def load_g(grp):
+            nc.sync.dma_start(
+                out=g_raw[grp][:], in_=g[512 * grp : 512 * grp + 512, :].rearrange("(p t) m -> p t m", t=4)
+            )
+
+        load_x(0, 0, 0, 2)
+        load_x(0, 1, 0, 2)
+        load_words(we_w, we_words, 0, FQ)
+        load_x(0, 0, 2, 4)
+        load_x(0, 1, 2, 4)
+        load_scales(nc.sync, we_s, we_scales)
+        nc.sync.dma_start(out=wt_sb[:], in_=wt.rearrange("(g p t) -> p g t", g=2, t=4))
+        load_words(we_w, we_words, FQ, F)
+        load_x(1, 0, 0, 4)
+        load_x(1, 1, 0, 4)
+        load_g(0)
+        load_g(1)
+        load_words(wd_w, wd_words, 0, F)
+        load_words(wn_w, wn_words, 0, M)
+        load_scales(nc.sync, wd_s, wd_scales)
+        load_scales(nc.sync, wn_s, wn_scales)
+        make_identity(nc, ident[:])
+
+        xt = {}
+        xg = {}
+
+        def x_transpose(k):
+            grp, t = divmod(k, 4)
+            bank = psum.tile([P, 2, 2, P], F32, name="m_bank", tag="m", bufs=M_BUFS)
+            xt[k] = bank
+            for s in (0, 1):
+                words = x_raw[grp, s][:, t, :].bitcast(F32)
+                for u in (0, 1):
+                    nc.tensor.transpose(bank[:, s, u, :], words[:, u : 2 * P : 2], ident[:])
+
+        def x_copy(k, on_scalar):
+            dst = work.tile([P, 2, P, 4], BF16, name="x_grouped", tag="x_grouped", bufs=3, align_bytes=64)
+            xg[k] = dst
+            out = dst[:].bitcast(F32)
+            src = xt[k][:].rearrange("p s u r -> p s r u")
+            if on_scalar:
+                nc.scalar.copy(out=out, in_=src)
+            else:
+                nc.vector.tensor_copy(out=out, in_=src)
+
+        def x_quant(k):
+            nc.vector.quantize_mx(
+                out=x_codes[k][:].bitcast(FP8X4),
+                scales=x_scales[k][:],
+                in_=xg[k][:].rearrange("p s r t -> p (s r t)"),
+            )
+
+        blocks = [(0, 256, 0), (256, 256, 0), (0, 256, 1), (256, 256, 1)]
+        blocks += [(512, 256, 0), (512, 256, 1), (768, 256, 0), (768, 128, 1), (896, 128, 1)]
+        units = []
+        for bi, (f0, fw, grp) in enumerate(blocks):
+            nt = 256 // fw
+            for t in range(0, 4, nt):
+                units.append((bi, t, nt))
+        last_unit = {}
+        for ui, (bi, t, nt) in enumerate(units):
+            last_unit[bi] = ui
+        hb, sg, zt = {}, {}, {}
+
+        def h_mm(u):
+            b, t0, nt = units[u]
+            f0, fw, grp = blocks[b]
+            bank = psum.tile([P, nt, 2, fw], F32, name="h_bank", tag="h", bufs=H_BUFS)
+            hb[u] = bank
+            for i in range(nt):
+                k = 4 * grp + t0 + i
+                for s in (0, 1):
+                    nc.tensor.matmul_mx(
+                        out=bank[:, i, s, :],
+                        lhsT=x_codes[k][:, s * P : s * P + P].bitcast(FP8X4),
+                        lhsT_scale=x_scales[k][:, s * P : s * P + P],
+                        rhs=we_w[:, f0 : f0 + fw].bitcast(FP8X4),
+                        rhs_scale=we_s[:, f0 : f0 + fw],
+                        start=True,
+                        stop=True,
+                    )
+
+        def sig(u):
+            b, t0, nt = units[u]
+            tile = work.tile([P, nt, 2, blocks[b][1]], F32, name="sig_t", tag="sig_t", bufs=SIG_BUFS, align_bytes=64)
+            sg[u] = tile
+            nc.scalar.activation(out=tile[:], in_=hb[u][:], func=ACT.Sigmoid, bias=-2.4, scale=8.0)
+
+        def stt(u):
+            b, t0, nt = units[u]
+            f0, fw, grp = blocks[b]
+            if t0 == 0:
+                zt[b] = work.tile([P, 4, 2, fw], F32, name="z_t", tag="z_t", bufs=3, align_bytes=64)
+            for i in range(nt):
+                t = t0 + i
+                nc.vector.scalar_tensor_tensor(
+                    out=zt[b][:, t, :, :],
+                    in0=hb[u][:, i, :, :],
+                    scalar=wt_sb[:, grp, t : t + 1],
+                    in1=sg[u][:, i, :, :],
+                    op0=ALU.mult,
+                    op1=ALU.mult,
+                )
+
+        dzb, dzc, dzs = {}, {}, {}
+
+        def sub(b, eng, j):
+            fw = blocks[b][1]
+            if b not in dzb:
+                dzb[b] = work.tile([P, fw, 4], BF16, name="dz_b", tag="dz_b", bufs=3, align_bytes=64)
+            cols = slice(j * P, j * P + P)
+            eng.tensor_tensor(
+                out=dzb[b][:, cols, :],
+                in0=zt[b][:, :, 1, cols].rearrange("p t f -> p f t"),
+                in1=zt[b][:, :, 0, cols].rearrange("p t f -> p f t"),
+                op=ALU.subtract,
+            )
+
+        def dz_quant(b):
+            fw = blocks[b][1]
+            dzc[b] = keep.tile([P, fw], U32, name="dz_codes_%d" % b, align_bytes=64)
+            dzs[b] = keep.tile([P, fw], U8, name="dz_scales_%d" % b, align_bytes=64)
+            nc.vector.quantize_mx(
+                out=dzc[b][:].bitcast(FP8X4), scales=dzs[b][:], in_=dzb[b][:].rearrange("p f t -> p (f t)")
+            )
+
+        gg = {}
+
+        def g_inter(grp, lo, hi, on_gpsimd):
+            if grp not in gg:
+                gg[grp] = keep.tile([P, M, 4], BF16, name="g_grouped_%d" % grp, align_bytes=64)
+            src = g_raw[grp][:, :, lo:hi].rearrange("p t m -> p m t")
+            if on_gpsimd:
+                nc.gpsimd.tensor_scalar(gg[grp][:, lo:hi, :], src, 1.0, 1.0, ALU.mult, ALU.mult)
+            else:
+                nc.vector.tensor_copy(out=gg[grp][:, lo:hi, :], in_=src)
+
+        def g_quant(grp):
+            nc.vector.quantize_mx(
+                out=g_codes[grp][:].bitcast(FP8X4),
+                scales=g_scales[grp][:],
+                in_=gg[grp][:].rearrange("p m t -> p (m t)"),
+            )
+
+        vb, nb, ot, ob = {}, {}, {}, {}
+
+        def v_mm(ft):
+            cols = slice(ft * P, ft * P + P)
+            bank = psum.tile([P, M], F32, name="m_bank", tag="m", bufs=M_BUFS)
+            vb[ft] = bank
+            nc.tensor.matmul_mx(
+                out=bank[:],
+                lhsT=wd_w[:, cols].bitcast(FP8X4),
+                lhsT_scale=wd_s[:, cols],
+                rhs=wn_w[:].bitcast(FP8X4),
+                rhs_scale=wn_s[:],
+                start=True,
+                stop=True,
+            )
+
+        def v_copy(ft):
+            nc.scalar.copy(out=v_sb[:, ft, :], in_=vb[ft][:])
+
+        def n_mm(ft, grps=(0, 1)):
+            if 0 in grps:
+                nb[ft] = psum.tile([P, M], F32, name="m_bank", tag="m", bufs=M_BUFS)
+            for grp in grps:
+                for b, (f0, fw, bg) in enumerate(blocks):
+                    if bg == grp and f0 <= ft * P < f0 + fw:
+                        cols = slice(ft * P - f0, ft * P - f0 + P)
+                        nc.tensor.matmul_mx(
+                            out=nb[ft][:],
+                            lhsT=dzc[b][:, cols].bitcast(FP8X4),
+                            lhsT_scale=dzs[b][:, cols],
+                            rhs=g_codes[grp][:].bitcast(FP8X4),
+                            rhs_scale=g_scales[grp][:],
+                            start=(grp == 0),
+                            stop=(grp == 1),
+                        )
+
+        def mult(ft):
+            tile = work.tile([P, M], F32, name="o_t", tag="o_t", bufs=4, align_bytes=64)
+            ot[ft] = tile
+            nc.vector.tensor_tensor(out=tile[:], in0=nb[ft][:], in1=v_sb[:, ft, :], op=ALU.mult)
+            nc.sync.dma_start(out=out_0[ft * P : ft * P + P, :], in_=tile[:])
+
+        def conv(ft, where):
+            tile = work.tile([P, M], BF16, name="o_b", tag="o_b", bufs=4, align_bytes=64)
+            ob[ft] = tile
+            if where == "g":
+                nc.gpsimd.tensor_scalar(tile[:], ot[ft][:], 1.0, 1.0, ALU.mult, ALU.mult)
+            elif where == "v":
+                nc.vector.tensor_copy(out=tile[:], in_=ot[ft][:])
+            else:
+                nc.scalar.copy(out=tile[:], in_=ot[ft][:])
+
+        pt, pb = {}, {}
+
+        def p_transpose(fts):
+            bank = psum.tile([P, len(fts), 2, P], F32, name="m_bank", tag="m", bufs=M_BUFS)
+            pt[fts] = bank
+            for j, ft in enumerate(fts):
+                words = ob[ft][:].bitcast(F32)
+                for u in (0, 1):
+                    nc.tensor.transpose(bank[:, j, u, :], words[:, u : 2 * P : 2], ident[:])
+
+        def p_copy(fts, where="s"):
+            dst = work.tile([P, len(fts), P, 4], BF16, name="p_grouped", tag="p_grouped", bufs=2, align_bytes=64)
+            pb[fts] = dst
+            src = pt[fts][:].rearrange("p j u f -> p j f u")
+            if where == "s":
+                nc.scalar.copy(out=dst[:].bitcast(F32), in_=src)
+            else:
+                nc.vector.tensor_copy(out=dst[:].bitcast(F32), in_=src)
+
+        def p_quant(fts):
+            lo, hi = fts[0] * P, fts[-1] * P + P
+            codes = work.tile([P, hi - lo], U32, name="p_codes", tag="p_codes", bufs=4, align_bytes=64)
+            nc.vector.quantize_mx(
+                out=codes[:].bitcast(FP8X4),
+                scales=p_scales[:, lo:hi],
+                in_=pb[fts][:].rearrange("p j f t -> p (j f t)"),
+            )
+            dst = out_1[0].rearrange("p n t -> p (n t)")[:, 4 * lo : 4 * hi]
+            nc.sync.dma_start(out=dst.bitcast(I32), in_=codes[:].bitcast(I32))
+
+        def p_scales_out(lo, hi):
+            for q in range(4):
+                nc.sync.dma_start(
+                    out=out_2[0, 4 * q : 4 * q + 4, lo:hi].bitcast(I32),
+                    in_=p_scales[32 * q : 32 * q + 4, lo:hi].bitcast(I32),
+                )
+
+        x_transpose(0)
+        x_transpose(1)
+        x_copy(0, True)
+        x_copy(1, False)
+        x_transpose(2)
+        x_transpose(3)
+        x_quant(0)
+        x_quant(1)
+        h_mm(0)
+        h_mm(1)
+        x_copy(2, True)
+        x_copy(3, False)
+        x_quant(2)
+        x_quant(3)
+        h_mm(2)
+
+        n_units = len(units)
+        for i in range(n_units + LAG):
+            if i < n_units:
+                sig(i)
+            w = i - LAG
+            if w >= 0:
+                stt(w)
+            if 3 <= w + LEAD < n_units:
+                h_mm(w + LEAD)
+            for k in range(4, 8):
+                at = TX + SX * (k - 4)
+                if i == at:
+                    x_transpose(k)
+                if i == at + 1:
+                    x_copy(k, k in XC_S)
+                if i == at + 2:
+                    x_quant(k)
+            for b in range(7):
+                if w == last_unit[b]:
+                    for j in (0, 1):
+                        sub(b, nc.vector if (b, j) in SUBV else nc.gpsimd, j)
+                    if b in (0, 1):
+                        g_inter(b, 0, 256, True)
+                        g_inter(b, 256, 512, True)
+                if w == last_unit[b] + DQ:
+                    dz_quant(b)
+            for grp in (0, 1):
+                if i == TGQ[grp]:
+                    g_quant(grp)
+            for ft in range(8):
+                if i == TV + SV * ft:
+                    v_mm(ft)
+                if i == TV + SV * ft + 1:
+                    v_copy(ft)
+            for fq, b in ((0, 2), (1, 3), (2, 5)):
+                d = w - last_unit[b] - DQ
+                fts = (2 * fq, 2 * fq + 1)
+                if d == D_N:
+                    n_mm(fts[0])
+                    n_mm(fts[1])
+                if d == D_M0:
+                    mult(fts[0])
+                if d == D_M1:
+                    mult(fts[1])
+                if d == D_C:
+                    conv(fts[0], CONV[fq])
+                    conv(fts[1], CONV[fq])
+                if d == D_T:
+                    p_transpose(fts)
+                if d == D_PC:
+                    p_copy(fts)
+                if d == D_PQ:
+                    p_quant(fts)
+            if w == last_unit[7]:
+                sub(7, nc.vector, 0)
+            if w == last_unit[7] + 1:
+                dz_quant(7)
+        late = (4, 5) not in pt
+        if 6 not in dzc:
+            dz_quant(6)
+        n_mm(6)
+        n_mm(7, (0,))
+        if late:
+            p_transpose((4, 5))
+            p_copy((4, 5))
+        sub(8, nc.vector, 0)
+        mult(6)
+        dz_quant(8)
+        n_mm(7, (1,))
+        conv(6, "s")
+        if late:
+            p_quant((4, 5))
+        p_scales_out(0, 768)
+        mult(7)
+        p_transpose((6,))
+        p_copy((6,))
+        conv(7, "v")
+        p_transpose((7,))
+        p_quant((6,))
+        p_copy((7,), "v")
+        p_quant((7,))
+        p_scales_out(768, 1024)

@@ -16,19 +16,21 @@ T, D, F, M = 1024, 512, 1024, 512
 FLOPS = 2 * (2 * T * D * F + T * F * M + F * D * M)
 P = 128
 FQ = 256
-H_BUFS = 4
-M_BUFS = 4
+H_BUFS = 5
+M_BUFS = 3
 SIG_BUFS = 4
 LEAD = 3
 LAG = 1
-TX, SX = 2, 1
-XC_S = (4, 5, 6, 7)
-TGQ = (11, 15)
+TX, SX = 4, 1
+XC_V = (1, 3)
 TV, SV = 8, 2
-DQ = 4
-CONV = ("g", "s", "s")
-D_N, D_M0, D_M1, D_C, D_T, D_PC, D_PQ = 1, 2, 3, 3, 6, 7, 8
-SUBV = ()
+D_N, D_M0, D_M1, D_C, D_T, D_PC, D_PQ = 1, 2, 3, 3, 5, 6, 8
+G_AT = ((2, "v", 0),)
+CONV = ("s", "s", "s")
+SUB_G = 192
+SUB_PIECES = 4
+DQLAG = 1
+BEFORE = 0
 
 
 def tile_smoothjumptranscoderedgeattribution_x2_kernel(
@@ -94,10 +96,10 @@ def tile_smoothjumptranscoderedgeattribution_x2_kernel(
         load_x(0, 1, 2, 4)
         load_scales(nc.sync, we_s, we_scales)
         nc.sync.dma_start(out=wt_sb[:], in_=wt.rearrange("(g p t) -> p g t", g=2, t=4))
+        load_g(0)
         load_words(we_w, we_words, FQ, F)
         load_x(1, 0, 0, 4)
         load_x(1, 1, 0, 4)
-        load_g(0)
         load_g(1)
         load_words(wd_w, wd_words, 0, F)
         load_words(wn_w, wn_words, 0, M)
@@ -134,8 +136,8 @@ def tile_smoothjumptranscoderedgeattribution_x2_kernel(
                 in_=xg[k][:].rearrange("p s r t -> p (s r t)"),
             )
 
-        blocks = [(0, 256, 0), (256, 256, 0), (0, 256, 1), (256, 256, 1)]
-        blocks += [(512, 256, 0), (512, 256, 1), (768, 256, 0), (768, 128, 1), (896, 128, 1)]
+        blocks = [(0, 256, 0), (256, 256, 0), (512, 256, 0), (0, 256, 1), (256, 256, 1), (512, 256, 1)]
+        blocks += [(768, 256, 0), (768, 128, 1), (896, 128, 1)]
         units = []
         for bi, (f0, fw, grp) in enumerate(blocks):
             nt = 256 // fw
@@ -188,17 +190,19 @@ def tile_smoothjumptranscoderedgeattribution_x2_kernel(
 
         dzb, dzc, dzs = {}, {}, {}
 
-        def sub(b, eng, j):
+        def sub(b, eng, lo, hi, pieces):
             fw = blocks[b][1]
             if b not in dzb:
                 dzb[b] = work.tile([P, fw, 4], BF16, name="dz_b", tag="dz_b", bufs=3, align_bytes=64)
-            cols = slice(j * P, j * P + P)
-            eng.tensor_tensor(
-                out=dzb[b][:, cols, :],
-                in0=zt[b][:, :, 1, cols].rearrange("p t f -> p f t"),
-                in1=zt[b][:, :, 0, cols].rearrange("p t f -> p f t"),
-                op=ALU.subtract,
-            )
+            n = (hi - lo) // pieces
+            for a in range(lo, hi, n):
+                cols = slice(a, a + n)
+                eng.tensor_tensor(
+                    out=dzb[b][:, cols, :].rearrange("p (c i) t -> p c t i", i=4),
+                    in0=zt[b][:, :, 1, cols].rearrange("p t (c i) -> p c t i", i=4),
+                    in1=zt[b][:, :, 0, cols].rearrange("p t (c i) -> p c t i", i=4),
+                    op=ALU.subtract,
+                )
 
         def dz_quant(b):
             fw = blocks[b][1]
@@ -210,14 +214,17 @@ def tile_smoothjumptranscoderedgeattribution_x2_kernel(
 
         gg = {}
 
-        def g_inter(grp, lo, hi, on_gpsimd):
+        def g_inter(grp, lo, hi, where):
             if grp not in gg:
                 gg[grp] = keep.tile([P, M, 4], BF16, name="g_grouped_%d" % grp, align_bytes=64)
-            src = g_raw[grp][:, :, lo:hi].rearrange("p t m -> p m t")
-            if on_gpsimd:
-                nc.gpsimd.tensor_scalar(gg[grp][:, lo:hi, :], src, 1.0, 1.0, ALU.mult, ALU.mult)
+            src = g_raw[grp][:, :, lo:hi].rearrange("p t (c i) -> p c t i", i=4)
+            dst = gg[grp][:, lo:hi, :].rearrange("p (c i) t -> p c t i", i=4)
+            if where == "g":
+                nc.gpsimd.tensor_scalar(dst, src, 1.0, 1.0, ALU.mult, ALU.mult)
+            elif where == "v":
+                nc.vector.tensor_copy(out=dst, in_=src)
             else:
-                nc.vector.tensor_copy(out=gg[grp][:, lo:hi, :], in_=src)
+                nc.scalar.copy(out=dst, in_=src)
 
         def g_quant(grp):
             nc.vector.quantize_mx(
@@ -331,13 +338,38 @@ def tile_smoothjumptranscoderedgeattribution_x2_kernel(
         x_quant(3)
         h_mm(2)
 
+        def boundary(w):
+            for b in range(7):
+                if w == last_unit[b]:
+                    c = b - DQLAG
+                    if c >= 0:
+                        if SUB_G < 256:
+                            sub(c, nc.vector, SUB_G, 256, 1)
+                    if b in (1, 2):
+                        x_quant(2 * b + 2)
+                        x_quant(2 * b + 3)
+                    if b == 2:
+                        g_inter(1, 0, 256, "v")
+                        g_inter(1, 256, 512, "v")
+                    if b in (2, 3):
+                        g_quant(b - 2)
+                    for fq in (0, 1, 2):
+                        if b == 4 + fq + 2:
+                            p_quant((2 * fq, 2 * fq + 1))
+                    if c >= 0:
+                        dz_quant(c)
+
         n_units = len(units)
         for i in range(n_units + LAG):
             if i < n_units:
                 sig(i)
             w = i - LAG
+            if w >= 0 and BEFORE:
+                boundary(w)
             if w >= 0:
                 stt(w)
+            if w >= 0 and not BEFORE:
+                boundary(w)
             if 3 <= w + LEAD < n_units:
                 h_mm(w + LEAD)
             for k in range(4, 8):
@@ -345,28 +377,22 @@ def tile_smoothjumptranscoderedgeattribution_x2_kernel(
                 if i == at:
                     x_transpose(k)
                 if i == at + 1:
-                    x_copy(k, k in XC_S)
-                if i == at + 2:
-                    x_quant(k)
-            for b in range(7):
-                if w == last_unit[b]:
-                    for j in (0, 1):
-                        sub(b, nc.vector if (b, j) in SUBV else nc.gpsimd, j)
-                    if b in (0, 1):
-                        g_inter(b, 0, 256, True)
-                        g_inter(b, 256, 512, True)
-                if w == last_unit[b] + DQ:
-                    dz_quant(b)
-            for grp in (0, 1):
-                if i == TGQ[grp]:
-                    g_quant(grp)
+                    x_copy(k, k not in XC_V)
+            for at, where, grp in G_AT:
+                for h in (0, 1):
+                    if i == at + h:
+                        g_inter(grp, 256 * h, 256 * h + 256, where)
             for ft in range(8):
                 if i == TV + SV * ft:
                     v_mm(ft)
                 if i == TV + SV * ft + 1:
                     v_copy(ft)
-            for fq, b in ((0, 2), (1, 3), (2, 5)):
-                d = w - last_unit[b] - DQ
+            for b in range(7):
+                if w == last_unit[b]:
+                    if SUB_G:
+                        sub(b, nc.gpsimd, 0, SUB_G, SUB_PIECES)
+            for fq in (0, 1, 2):
+                d = w - last_unit[4 + fq]
                 fts = (2 * fq, 2 * fq + 1)
                 if d == D_N:
                     n_mm(fts[0])
@@ -377,32 +403,35 @@ def tile_smoothjumptranscoderedgeattribution_x2_kernel(
                     mult(fts[1])
                 if d == D_C:
                     conv(fts[0], CONV[fq])
+                if d == D_C + 1:
                     conv(fts[1], CONV[fq])
                 if d == D_T:
                     p_transpose(fts)
                 if d == D_PC:
                     p_copy(fts)
-                if d == D_PQ:
-                    p_quant(fts)
-            if w == last_unit[7]:
-                sub(7, nc.vector, 0)
-            if w == last_unit[7] + 1:
-                dz_quant(7)
-        late = (4, 5) not in pt
-        if 6 not in dzc:
-            dz_quant(6)
-        n_mm(6)
+            if w == last_unit[8]:
+                sub(7, nc.vector, 0, 128, 1)
+        for b in range(7):
+            if b not in dzc:
+                if SUB_G < 256:
+                    sub(b, nc.vector, SUB_G, 256, 1)
+                dz_quant(b)
+        n_mm(6, (0,))
         n_mm(7, (0,))
-        if late:
-            p_transpose((4, 5))
-            p_copy((4, 5))
-        sub(8, nc.vector, 0)
-        mult(6)
+        sub(8, nc.vector, 0, 128, 1)
+        dz_quant(7)
+        n_mm(6, (1,))
+        p_quant((2, 3))
         dz_quant(8)
         n_mm(7, (1,))
+        for fts in ((4, 5),):
+            if fts not in pt:
+                p_transpose(fts)
+            if fts not in pb:
+                p_copy(fts)
+        mult(6)
+        p_quant((4, 5))
         conv(6, "s")
-        if late:
-            p_quant((4, 5))
         p_scales_out(0, 768)
         mult(7)
         p_transpose((6,))

from contextlib import ExitStack

import concourse.mybir as mybir
from concourse.masks import make_identity

F32 = mybir.dt.float32
BF16 = mybir.dt.bfloat16
I32 = mybir.dt.int32
U32 = mybir.dt.uint32
U8 = mybir.dt.uint8
FP8X4 = mybir.dt.float8_e4m3fn_x4
ALU = mybir.AluOpType
ACT = mybir.ActivationFunctionType

T, D, F, M = 1024, 512, 1024, 512
FLOPS = 2 * (2 * T * D * F + T * F * M + F * D * M)
P = 128
FQ = 256
H_BUFS = 5
M_BUFS = 3
SIG_BUFS = 4
LEAD = 3
LAG = 1
TX, SX = 4, 1
XC_V = (1, 3)
TV, SV = 8, 2
D_N, D_M0, D_M1, D_C, D_T, D_PC, D_PQ = 1, 2, 3, 3, 5, 6, 8
G_AT = ((2, "v", 0),)
CONV = ("s", "s", "s")
SUB_G = 192
SUB_PIECES = 4
DQLAG = 1
BEFORE = 0


def tile_smoothjumptranscoderedgeattribution_x2_kernel(
    tc, xc, xr, we_words, we_scales, wt, g, wd_words, wd_scales, wn_words, wn_scales, out_0, out_1, out_2
):
    nc = tc.nc
    with ExitStack() as ctx:
        keep = ctx.enter_context(tc.tile_pool(name="keep", bufs=1))
        work = ctx.enter_context(tc.tile_pool(name="work", bufs=3))
        psum = ctx.enter_context(tc.psum_pool(name="psum", bufs=2))
        ctx.enter_context(tc.manual_schedule())

        x_raw = {}
        for grp in (0, 1):
            for s in (0, 1):
                x_raw[grp, s] = keep.tile([P, 4, D], BF16, name="x_raw_%d_%d" % (grp, s), align_bytes=64)
        g_raw = [keep.tile([P, 4, M], BF16, name="g_raw_%d" % i, align_bytes=64) for i in (0, 1)]
        we_w = keep.tile([P, F], U32, name="we_w", align_bytes=64)
        we_s = keep.tile([P, F], U8, name="we_s", align_bytes=64)
        wd_w = keep.tile([P, F], U32, name="wd_w", align_bytes=64)
        wd_s = keep.tile([P, F], U8, name="wd_s", align_bytes=64)
        wn_w = keep.tile([P, M], U32, name="wn_w", align_bytes=64)
        wn_s = keep.tile([P, M], U8, name="wn_s", align_bytes=64)
        wt_sb = keep.tile([P, 2, 4], BF16, name="wt_sb", align_bytes=64)
        ident = keep.tile([P, P], F32, name="ident", align_bytes=64)
        warm = keep.tile([P, 1], F32, name="warm", align_bytes=64)
        v_sb = keep.tile([P, 8, M], F32, name="v_sb", align_bytes=64)
        p_scales = keep.tile([P, F], U8, name="p_scales", align_bytes=64)
        g_codes = [keep.tile([P, M], U32, name="g_codes_%d" % i, align_bytes=64) for i in (0, 1)]
        g_scales = [keep.tile([P, M], U8, name="g_scales_%d" % i, align_bytes=64) for i in (0, 1)]
        x_codes = [keep.tile([P, 2 * P], U32, name="x_codes_%d" % i, align_bytes=64) for i in range(8)]
        x_scales = [keep.tile([P, 2 * P], U8, name="x_scales_%d" % i, align_bytes=64) for i in range(8)]

        nc.vector.memset(we_s[:].bitcast(I32), 0)
        nc.vector.memset(wd_s[:].bitcast(I32), 0)
        nc.vector.memset(wn_s[:].bitcast(I32), 0)
        nc.vector.memset(warm[:], 0.0)
        nc.scalar.activation(out=warm[:], in_=warm[:], func=ACT.Sigmoid)

        def load_x(grp, s, t0, t1):
            src = (xc, xr)[s][512 * grp : 512 * grp + 512, :].rearrange("(p t) d -> p t d", t=4)
            nc.sync.dma_start(out=x_raw[grp, s][:, t0:t1, :], in_=src[:, t0:t1, :])

        def load_words(tile, dram, a, b):
            src = dram[0].rearrange("p n t -> p (n t)")[:, 4 * a : 4 * b]
            nc.sync.dma_start(out=tile[:, a:b].bitcast(I32), in_=src.bitcast(I32))

        def load_scales(eng, tile, dram):
            for q in range(4):
                eng.dma_start(
                    out=tile[32 * q : 32 * q + 4, :].bitcast(I32), in_=dram[0, 4 * q : 4 * q + 4, :].bitcast(I32)
                )

        def load_g(grp):
            nc.sync.dma_start(
                out=g_raw[grp][:], in_=g[512 * grp : 512 * grp + 512, :].rearrange("(p t) m -> p t m", t=4)
            )

        load_x(0, 0, 0, 2)
        load_x(0, 1, 0, 2)
        load_words(we_w, we_words, 0, FQ)
        load_x(0, 0, 2, 4)
        load_x(0, 1, 2, 4)
        load_scales(nc.sync, we_s, we_scales)
        nc.sync.dma_start(out=wt_sb[:], in_=wt.rearrange("(g p t) -> p g t", g=2, t=4))
        load_g(0)
        load_words(we_w, we_words, FQ, F)
        load_x(1, 0, 0, 4)
        load_x(1, 1, 0, 4)
        load_g(1)
        load_words(wd_w, wd_words, 0, F)
        load_words(wn_w, wn_words, 0, M)
        load_scales(nc.sync, wd_s, wd_scales)
        load_scales(nc.sync, wn_s, wn_scales)
        make_identity(nc, ident[:])

        xt = {}
        xg = {}

        def x_transpose(k):
            grp, t = divmod(k, 4)
            bank = psum.tile([P, 2, 2, P], F32, name="m_bank", tag="m", bufs=M_BUFS)
            xt[k] = bank
            for s in (0, 1):
                words = x_raw[grp, s][:, t, :].bitcast(F32)
                for u in (0, 1):
                    nc.tensor.transpose(bank[:, s, u, :], words[:, u : 2 * P : 2], ident[:])

        def x_copy(k, on_scalar):
            dst = work.tile([P, 2, P, 4], BF16, name="x_grouped", tag="x_grouped", bufs=3, align_bytes=64)
            xg[k] = dst
            out = dst[:].bitcast(F32)
            src = xt[k][:].rearrange("p s u r -> p s r u")
            if on_scalar:
                nc.scalar.copy(out=out, in_=src)
            else:
                nc.vector.tensor_copy(out=out, in_=src)

        def x_quant(k):
            nc.vector.quantize_mx(
                out=x_codes[k][:].bitcast(FP8X4),
                scales=x_scales[k][:],
                in_=xg[k][:].rearrange("p s r t -> p (s r t)"),
            )

        blocks = [(0, 256, 0), (256, 256, 0), (512, 256, 0), (0, 256, 1), (256, 256, 1), (512, 256, 1)]
        blocks += [(768, 256, 0), (768, 128, 1), (896, 128, 1)]
        units = []
        for bi, (f0, fw, grp) in enumerate(blocks):
            nt = 256 // fw
            for t in range(0, 4, nt):
                units.append((bi, t, nt))
        last_unit = {}
        for ui, (bi, t, nt) in enumerate(units):
            last_unit[bi] = ui
        hb, sg, zt = {}, {}, {}

        def h_mm(u):
            b, t0, nt = units[u]
            f0, fw, grp = blocks[b]
            bank = psum.tile([P, nt, 2, fw], F32, name="h_bank", tag="h", bufs=H_BUFS)
            hb[u] = bank
            for i in range(nt):
                k = 4 * grp + t0 + i
                for s in (0, 1):
                    nc.tensor.matmul_mx(
                        out=bank[:, i, s, :],
                        lhsT=x_codes[k][:, s * P : s * P + P].bitcast(FP8X4),
                        lhsT_scale=x_scales[k][:, s * P : s * P + P],
                        rhs=we_w[:, f0 : f0 + fw].bitcast(FP8X4),
                        rhs_scale=we_s[:, f0 : f0 + fw],
                        start=True,
                        stop=True,
                    )

        def sig(u):
            b, t0, nt = units[u]
            tile = work.tile([P, nt, 2, blocks[b][1]], F32, name="sig_t", tag="sig_t", bufs=SIG_BUFS, align_bytes=64)
            sg[u] = tile
            nc.scalar.activation(out=tile[:], in_=hb[u][:], func=ACT.Sigmoid, bias=-2.4, scale=8.0)

        def stt(u):
            b, t0, nt = units[u]
            f0, fw, grp = blocks[b]
            if t0 == 0:
                zt[b] = work.tile([P, 4, 2, fw], F32, name="z_t", tag="z_t", bufs=3, align_bytes=64)
            for i in range(nt):
                t = t0 + i
                nc.vector.scalar_tensor_tensor(
                    out=zt[b][:, t, :, :],
                    in0=hb[u][:, i, :, :],
                    scalar=wt_sb[:, grp, t : t + 1],
                    in1=sg[u][:, i, :, :],
                    op0=ALU.mult,
                    op1=ALU.mult,
                )

        dzb, dzc, dzs = {}, {}, {}

        def sub(b, eng, lo, hi, pieces):
            fw = blocks[b][1]
            if b not in dzb:
                dzb[b] = work.tile([P, fw, 4], BF16, name="dz_b", tag="dz_b", bufs=3, align_bytes=64)
            n = (hi - lo) // pieces
            for a in range(lo, hi, n):
                cols = slice(a, a + n)
                eng.tensor_tensor(
                    out=dzb[b][:, cols, :].rearrange("p (c i) t -> p c t i", i=4),
                    in0=zt[b][:, :, 1, cols].rearrange("p t (c i) -> p c t i", i=4),
                    in1=zt[b][:, :, 0, cols].rearrange("p t (c i) -> p c t i", i=4),
                    op=ALU.subtract,
                )

        def dz_quant(b):
            fw = blocks[b][1]
            dzc[b] = keep.tile([P, fw], U32, name="dz_codes_%d" % b, align_bytes=64)
            dzs[b] = keep.tile([P, fw], U8, name="dz_scales_%d" % b, align_bytes=64)
            nc.vector.quantize_mx(
                out=dzc[b][:].bitcast(FP8X4), scales=dzs[b][:], in_=dzb[b][:].rearrange("p f t -> p (f t)")
            )

        gg = {}

        def g_inter(grp, lo, hi, where):
            if grp not in gg:
                gg[grp] = keep.tile([P, M, 4], BF16, name="g_grouped_%d" % grp, align_bytes=64)
            src = g_raw[grp][:, :, lo:hi].rearrange("p t (c i) -> p c t i", i=4)
            dst = gg[grp][:, lo:hi, :].rearrange("p (c i) t -> p c t i", i=4)
            if where == "g":
                nc.gpsimd.tensor_scalar(dst, src, 1.0, 1.0, ALU.mult, ALU.mult)
            elif where == "v":
                nc.vector.tensor_copy(out=dst, in_=src)
            else:
                nc.scalar.copy(out=dst, in_=src)

        def g_quant(grp):
            nc.vector.quantize_mx(
                out=g_codes[grp][:].bitcast(FP8X4),
                scales=g_scales[grp][:],
                in_=gg[grp][:].rearrange("p m t -> p (m t)"),
            )

        vb, nb, ot, ob = {}, {}, {}, {}

        def v_mm(ft):
            cols = slice(ft * P, ft * P + P)
            bank = psum.tile([P, M], F32, name="m_bank", tag="m", bufs=M_BUFS)
            vb[ft] = bank
            nc.tensor.matmul_mx(
                out=bank[:],
                lhsT=wd_w[:, cols].bitcast(FP8X4),
                lhsT_scale=wd_s[:, cols],
                rhs=wn_w[:].bitcast(FP8X4),
                rhs_scale=wn_s[:],
                start=True,
                stop=True,
            )

        def v_copy(ft):
            nc.scalar.copy(out=v_sb[:, ft, :], in_=vb[ft][:])

        def n_mm(ft, grps=(0, 1)):
            if 0 in grps:
                nb[ft] = psum.tile([P, M], F32, name="m_bank", tag="m", bufs=M_BUFS)
            for grp in grps:
                for b, (f0, fw, bg) in enumerate(blocks):
                    if bg == grp and f0 <= ft * P < f0 + fw:
                        cols = slice(ft * P - f0, ft * P - f0 + P)
                        nc.tensor.matmul_mx(
                            out=nb[ft][:],
                            lhsT=dzc[b][:, cols].bitcast(FP8X4),
                            lhsT_scale=dzs[b][:, cols],
                            rhs=g_codes[grp][:].bitcast(FP8X4),
                            rhs_scale=g_scales[grp][:],
                            start=(grp == 0),
                            stop=(grp == 1),
                        )

        def mult(ft):
            tile = work.tile([P, M], F32, name="o_t", tag="o_t", bufs=4, align_bytes=64)
            ot[ft] = tile
            nc.vector.tensor_tensor(out=tile[:], in0=nb[ft][:], in1=v_sb[:, ft, :], op=ALU.mult)
            nc.sync.dma_start(out=out_0[ft * P : ft * P + P, :], in_=tile[:])

        def conv(ft, where):
            tile = work.tile([P, M], BF16, name="o_b", tag="o_b", bufs=4, align_bytes=64)
            ob[ft] = tile
            if where == "g":
                nc.gpsimd.tensor_scalar(tile[:], ot[ft][:], 1.0, 1.0, ALU.mult, ALU.mult)
            elif where == "v":
                nc.vector.tensor_copy(out=tile[:], in_=ot[ft][:])
            else:
                nc.scalar.copy(out=tile[:], in_=ot[ft][:])

        pt, pb = {}, {}

        def p_transpose(fts):
            bank = psum.tile([P, len(fts), 2, P], F32, name="m_bank", tag="m", bufs=M_BUFS)
            pt[fts] = bank
            for j, ft in enumerate(fts):
                words = ob[ft][:].bitcast(F32)
                for u in (0, 1):
                    nc.tensor.transpose(bank[:, j, u, :], words[:, u : 2 * P : 2], ident[:])

        def p_copy(fts, where="s"):
            dst = work.tile([P, len(fts), P, 4], BF16, name="p_grouped", tag="p_grouped", bufs=2, align_bytes=64)
            pb[fts] = dst
            src = pt[fts][:].rearrange("p j u f -> p j f u")
            if where == "s":
                nc.scalar.copy(out=dst[:].bitcast(F32), in_=src)
            else:
                nc.vector.tensor_copy(out=dst[:].bitcast(F32), in_=src)

        def p_quant(fts):
            lo, hi = fts[0] * P, fts[-1] * P + P
            codes = work.tile([P, hi - lo], U32, name="p_codes", tag="p_codes", bufs=4, align_bytes=64)
            nc.vector.quantize_mx(
                out=codes[:].bitcast(FP8X4),
                scales=p_scales[:, lo:hi],
                in_=pb[fts][:].rearrange("p j f t -> p (j f t)"),
            )
            dst = out_1[0].rearrange("p n t -> p (n t)")[:, 4 * lo : 4 * hi]
            nc.sync.dma_start(out=dst.bitcast(I32), in_=codes[:].bitcast(I32))

        def p_scales_out(lo, hi):
            for q in range(4):
                nc.sync.dma_start(
                    out=out_2[0, 4 * q : 4 * q + 4, lo:hi].bitcast(I32),
                    in_=p_scales[32 * q : 32 * q + 4, lo:hi].bitcast(I32),
                )

        x_transpose(0)
        x_transpose(1)
        x_copy(0, True)
        x_copy(1, False)
        x_transpose(2)
        x_transpose(3)
        x_quant(0)
        x_quant(1)
        h_mm(0)
        h_mm(1)
        x_copy(2, True)
        x_copy(3, False)
        x_quant(2)
        x_quant(3)
        h_mm(2)

        def boundary(w):
            for b in range(7):
                if w == last_unit[b]:
                    c = b - DQLAG
                    if c >= 0:
                        if SUB_G < 256:
                            sub(c, nc.vector, SUB_G, 256, 1)
                    if b in (1, 2):
                        x_quant(2 * b + 2)
                        x_quant(2 * b + 3)
                    if b == 2:
                        g_inter(1, 0, 256, "v")
                        g_inter(1, 256, 512, "v")
                    if b in (2, 3):
                        g_quant(b - 2)
                    for fq in (0, 1, 2):
                        if b == 4 + fq + 2:
                            p_quant((2 * fq, 2 * fq + 1))
                    if c >= 0:
                        dz_quant(c)

        n_units = len(units)
        for i in range(n_units + LAG):
            if i < n_units:
                sig(i)
            w = i - LAG
            if w >= 0 and BEFORE:
                boundary(w)
            if w >= 0:
                stt(w)
            if w >= 0 and not BEFORE:
                boundary(w)
            if 3 <= w + LEAD < n_units:
                h_mm(w + LEAD)
            for k in range(4, 8):
                at = TX + SX * (k - 4)
                if i == at:
                    x_transpose(k)
                if i == at + 1:
                    x_copy(k, k not in XC_V)
            for at, where, grp in G_AT:
                for h in (0, 1):
                    if i == at + h:
                        g_inter(grp, 256 * h, 256 * h + 256, where)
            for ft in range(8):
                if i == TV + SV * ft:
                    v_mm(ft)
                if i == TV + SV * ft + 1:
                    v_copy(ft)
            for b in range(7):
                if w == last_unit[b]:
                    if SUB_G:
                        sub(b, nc.gpsimd, 0, SUB_G, SUB_PIECES)
            for fq in (0, 1, 2):
                d = w - last_unit[4 + fq]
                fts = (2 * fq, 2 * fq + 1)
                if d == D_N:
                    n_mm(fts[0])
                    n_mm(fts[1])
                if d == D_M0:
                    mult(fts[0])
                if d == D_M1:
                    mult(fts[1])
                if d == D_C:
                    conv(fts[0], CONV[fq])
                if d == D_C + 1:
                    conv(fts[1], CONV[fq])
                if d == D_T:
                    p_transpose(fts)
                if d == D_PC:
                    p_copy(fts)
            if w == last_unit[8]:
                sub(7, nc.vector, 0, 128, 1)
        for b in range(7):
            if b not in dzc:
                if SUB_G < 256:
                    sub(b, nc.vector, SUB_G, 256, 1)
                dz_quant(b)
        n_mm(6, (0,))
        n_mm(7, (0,))
        sub(8, nc.vector, 0, 128, 1)
        dz_quant(7)
        n_mm(6, (1,))
        p_quant((2, 3))
        dz_quant(8)
        n_mm(7, (1,))
        for fts in ((4, 5),):
            if fts not in pt:
                p_transpose(fts)
            if fts not in pb:
                p_copy(fts)
        mult(6)
        p_quant((4, 5))
        conv(6, "s")
        p_scales_out(0, 768)
        mult(7)
        p_transpose((6,))
        p_copy((6,))
        conv(7, "v")
        p_transpose((7,))
        p_quant((6,))
        p_copy((7,), "v")
        p_quant((7,))
        p_scales_out(768, 1024)
